import numpy as np
import ml_dtypes


def mxq(x, axis, fmt="e4m3"):
    dtype, down = {"e4m3": (ml_dtypes.float8_e4m3fn, 7), "e5m2": (ml_dtypes.float8_e5m2, 14)}[fmt]
    v = np.moveaxis(np.asarray(x, np.float32).astype(ml_dtypes.bfloat16).astype(np.float64), axis, -1)
    blocks = v.reshape(v.shape[:-1] + (-1, 32))
    amax = np.abs(blocks).max(-1, keepdims=True)
    byte = np.maximum(np.where(amax > 0, np.frexp(amax)[1] - 1 + 127, 0) - down, 1)
    scale = np.exp2(byte - 127.0)
    codes = (blocks / scale).astype(np.float32).astype(dtype).astype(np.float64)
    return np.moveaxis((codes * scale).reshape(v.shape), -1, axis)


WIDE = False


def mx_kscale(k):
    if not WIDE:
        return np.ones(k)
    levels = np.array([10, -10, 5, -5, 0])
    if k % 512:
        return np.exp2(np.random.permutation(np.resize(levels, k // 32))).repeat(32)
    a = np.empty((k // 512, 16))
    for p in range(k // 512):
        a[p, :8] = np.random.permutation(np.resize(levels, 8))
        for g in range(8):
            far = levels[np.abs(levels - a[p, g]) >= 10]
            a[p, g + 8] = far[np.random.randint(len(far))]
    return np.exp2(a.ravel()).repeat(32)


def f64(x):
    return np.asarray(x).astype(np.float64)


def striped(idx):
    return np.tile(idx.reshape(-1, 16).T, (8, 1)).astype(np.uint16)


def unstriped(offs):
    return offs[:16].T.reshape(-1).astype(np.int64)


def pack_weight(w):
    k, n = w.shape
    w = f64(np.asarray(w, np.float32).astype(ml_dtypes.bfloat16)).reshape(k // 32, 32, n)
    amax = np.abs(w).max(1)
    byte = np.clip(np.where(amax > 0, np.frexp(amax)[1] - 1 + 127 - 7, 1), 1, 254)
    scaled = (w * np.exp2(127.0 - byte)[:, None, :]).reshape(k, n).astype(np.float32)
    words = np.ascontiguousarray(scaled.reshape(k // 512, 128, 4, n).transpose(0, 1, 3, 2)).astype(ml_dtypes.float8_e4m3fn).view(np.uint8)
    return words, np.ascontiguousarray(byte.astype(np.uint8).reshape(k // 512, 16, n))


def unpack_weight(words, scales):
    g, p, n, _ = words.shape
    vals = np.ascontiguousarray(words).view(ml_dtypes.float8_e4m3fn).astype(np.float64) * np.repeat(np.exp2(scales.astype(np.float64) - 127.0), 8, axis=1)[..., None]
    return vals.transpose(0, 1, 3, 2).reshape(g * 512, n)


def planes(y):
    n, m = y.shape
    v = y.astype(np.float32).astype(ml_dtypes.bfloat16).astype(np.float64).reshape(n // 32, 32, m)
    top = np.abs(v).max(1)
    byte = np.clip(np.where(top > 0, np.frexp(top)[1] - 1 + 127 - 7, 1), 1, 254)
    codes = (v * np.exp2(127.0 - byte)[:, None, :]).reshape(n, m).astype(np.float32).astype(ml_dtypes.float8_e4m3fn).view(np.uint8)
    words = codes.reshape(n // 512, 128, 4, m).transpose(0, 1, 3, 2)
    return np.ascontiguousarray(words), np.ascontiguousarray(byte.astype(np.uint8).reshape(n // 512, 16, m))


K, T, S, N, H, W, U = 512, 2048, 512, 512, 512, 1024, 1024


def setup_inputs():
    n = np.random.standard_normal
    s = mx_kscale(K)[:, None]
    u = mx_kscale(H)
    packed_xT = pack_weight(n((K, T)) * s)
    packed_eT = pack_weight(n((K, W)) * s)
    return {
        "x_words": packed_xT[0],
        "x_scales": packed_xT[1],
        "w1": (n((K, N)) / np.sqrt(K) / s).astype(np.float32),
        "e_words": packed_eT[0],
        "e_scales": packed_eT[1],
        "w2": (n((K, N)) / np.sqrt(K) / s).astype(np.float32),
        "unit": (np.random.uniform(0.6, 1.4, (H, 1)) * u[:, None]).astype(np.float32),
        "w3": (n((H, N)) / np.sqrt(H) / u[:, None]).astype(np.float32),
        "offs": striped(np.random.permutation(T)[:S]),
        "wrd": striped(np.random.permutation(W)[:S]),
        "t1": striped(np.random.permutation(np.concatenate([np.arange(S), np.random.randint(0, S, U - S)]))),
        "t2": striped(np.random.permutation(np.concatenate([np.arange(S), np.random.randint(0, S, U - S)]))),
        "qw": striped(np.random.permutation(np.concatenate([np.arange(S), np.random.randint(0, S, U - S)]))),
    }


def reference(x_words, x_scales, w1, e_words, e_scales, w2, unit, w3, offs, wrd, t1, t2, qw):
    xq = unpack_weight(x_words, x_scales)[:, unstriped(offs)]
    y = mxq(f64(w1), 0, "e4m3").T @ xq
    y_1 = y[:, unstriped(t1)]
    y_2 = y[:, unstriped(t2)]
    per = np.maximum(y_1, y_2)
    e_wrd = unpack_weight(e_words, e_scales)[:, unstriped(wrd)]
    ye = mxq(f64(w2), 0, "e4m3").T @ e_wrd
    eq_ = ye[:, unstriped(qw)]
    fq = per + eq_
    hid = f64(unit) * (fq * y_1)
    out_0 = mxq(f64(w3), 0, "e4m3").T @ mxq(hid, 0, "e4m3")
    return (out_0,) + planes(out_0)

@@ -1,0 +1,213 @@
+from contextlib import ExitStack
+
+import concourse.mybir as mybir
+
+K, T, S, N, H, W, U = 512, 2048, 512, 512, 512, 1024, 1024
+FLOPS = 2 * K * N * S * 2 + 2 * H * N * U
+
+F32 = mybir.dt.float32
+BF16 = mybir.dt.bfloat16
+I32 = mybir.dt.int32
+U32 = mybir.dt.uint32
+U16 = mybir.dt.uint16
+U8 = mybir.dt.uint8
+FP8X4 = mybir.dt.float8_e4m3fn_x4
+ALU = mybir.AluOpType
+ACT = mybir.ActivationFunctionType
+
+P = 128
+PACK = 4
+CHUNKS = (256, 256, 256, 256)
+
+
+def tile_picked_yvideoq_per_po_kernel(
+    tc, x_words, x_scales, w1, e_words, e_scales, w2, unit, w3, offs, wrd, t1, t2, qw, out_0, out_1, out_2
+):
+    nc = tc.nc
+    with ExitStack() as ctx:
+        lists = ctx.enter_context(tc.tile_pool(name="lists", bufs=1))
+        keep = ctx.enter_context(tc.tile_pool(name="keep", bufs=1))
+        work = ctx.enter_context(tc.tile_pool(name="work", bufs=2))
+        psum = ctx.enter_context(tc.psum_pool(name="psum", bufs=8))
+
+        def load_list(src, name):
+            tile = lists.tile(list(src.shape), U16, name=name)
+            nc.sync.dma_start(tile[:], src)
+            return tile
+
+        def load_weight(src, name):
+            raw = keep.tile([P, PACK, N], F32, name=name)
+            nc.sync.dma_start(raw[:], src.rearrange("(p j) n -> p j n", j=PACK))
+            return raw
+
+        def load_words(src, width, name):
+            table = keep.tile([P, width], I32, name=name)
+            nc.sync.dma_start(table[:], src[0].rearrange("p n t -> p (n t)").bitcast(I32))
+            return table
+
+        def load_scales(src, width, name, queue):
+            table = keep.tile([P, width], U8, name=name)
+            nc.vector.memset(table[:].bitcast(I32), 0)
+            for q in range(4):
+                queue.dma_start(table[32 * q : 32 * q + 4, :].bitcast(I32), src[0, 4 * q : 4 * q + 4, :].bitcast(I32))
+            return table
+
+        def pick(table_view, offsets, dtype, name):
+            picked = keep.tile([P, S], dtype, name=name, align_bytes=64)
+            nc.vector.tensor_copy(picked[:], table_view.indirect(offsets[:]))
+            return picked
+
+        def round_weight_half(raw, half, copy, name):
+            grouped = keep.tile([P, 2 * P * PACK], BF16, name=name, align_bytes=64)
+            copy(
+                grouped[:].rearrange("p (e m j) -> p m j e", e=2, j=PACK),
+                raw[:].rearrange("p j (m u e) -> p u m j e", u=2, e=2)[:, half],
+            )
+            return grouped
+
+        def quantize_weight_half(grouped, name):
+            codes = keep.tile([P, 2 * P], U32, name=name + "_codes", align_bytes=64)
+            scales = keep.tile([P, 2 * P], U8, name=name + "_scales", align_bytes=64)
+            nc.vector.quantize_mx(out=codes[:].bitcast(FP8X4), scales=scales[:], in_=grouped[:])
+            return codes, scales
+
+        def product(out, halves, t, codes, scales):
+            w_codes, w_scales = halves[t // 2]
+            cols = slice((t % 2) * P, (t % 2 + 1) * P)
+            nc.tensor.matmul_mx(
+                out=out,
+                lhsT=w_codes[:, cols].bitcast(FP8X4),
+                lhsT_scale=w_scales[:, cols],
+                rhs=codes.bitcast(FP8X4),
+                rhs_scale=scales,
+                start=True,
+                stop=True,
+            )
+
+        offs_list = load_list(offs, "offs_list")
+        w1_raw = load_weight(w1, "w1_raw")
+        x_scale_table = load_scales(x_scales, T, "x_scale_table", nc.sync)
+        unit_tile = keep.tile([P, PACK], F32, name="unit_tile")
+        nc.sync.dma_start(unit_tile[:], unit.rearrange("(p t) o -> p (t o)", t=PACK))
+        wrd_list = load_list(wrd, "wrd_list")
+        x_word_table = load_words(x_words, T, "x_word_table")
+        e_word_table = load_words(e_words, W, "e_word_table")
+        e_scale_table = load_scales(e_scales, W, "e_scale_table", nc.sync)
+        t1_list = load_list(t1, "t1_list")
+        w2_raw = load_weight(w2, "w2_raw")
+        t2_list = load_list(t2, "t2_list")
+        qw_list = load_list(qw, "qw_list")
+        w3_raw = load_weight(w3, "w3_raw")
+
+        unit_sign = keep.tile([P, PACK], F32, name="unit_sign")
+        unit_abs = keep.tile([P, PACK], F32, name="unit_abs")
+        nc.scalar.activation(unit_sign[:], unit_tile[:], ACT.Sign)
+        nc.scalar.activation(unit_abs[:], unit_tile[:], ACT.Abs)
+
+        w1_grouped = [
+            round_weight_half(w1_raw, 0, nc.scalar.copy, "w1_grouped0"),
+            round_weight_half(w1_raw, 1, nc.scalar.copy, "w1_grouped1"),
+        ]
+        w1_halves = [quantize_weight_half(w1_grouped[h], "w1_%d" % h) for h in range(2)]
+        x_codes = pick(x_word_table[:].bitcast(U32), offs_list, U32, "x_codes")
+        x_bytes = pick(x_scale_table[:], offs_list, U8, "x_bytes")
+        y_signed, y_scaled, ye_scaled = [], [], []
+        for t in range(PACK):
+            bank = psum.tile([P, S], F32, name="bank")
+            product(bank[:], w1_halves, t, x_codes[:], x_bytes[:])
+            y_signed.append(keep.tile([P, S], F32, name="y_signed%d" % t, align_bytes=64))
+            nc.scalar.activation(y_signed[t][:], bank[:], ACT.Copy, scale=unit_sign[:, t : t + 1])
+            y_scaled.append(keep.tile([P, S], F32, name="y_scaled%d" % t, align_bytes=64))
+            nc.vector.tensor_scalar(y_scaled[t][:], y_signed[t][:], unit_tile[:, t : t + 1], None, ALU.mult)
+
+        e_bytes = pick(e_scale_table[:], wrd_list, U8, "e_bytes")
+        e_codes = pick(e_word_table[:].bitcast(U32), wrd_list, U32, "e_codes")
+        w2_grouped = [round_weight_half(w2_raw, h, nc.vector.tensor_copy, "w2_grouped%d" % h) for h in range(2)]
+        w2_halves = [quantize_weight_half(w2_grouped[h], "w2_%d" % h) for h in range(2)]
+        for t in range(PACK):
+            bank = psum.tile([P, S], F32, name="bank")
+            product(bank[:], w2_halves, t, e_codes[:], e_bytes[:])
+            ye_scaled.append(keep.tile([P, S], F32, name="ye_scaled%d" % t, align_bytes=64))
+            if t < 2:
+                nc.vector.tensor_scalar(ye_scaled[t][:], bank[:], unit_abs[:, t : t + 1], None, ALU.mult)
+            else:
+                nc.scalar.activation(ye_scaled[t][:], bank[:], ACT.Copy, scale=unit_abs[:, t : t + 1])
+
+        out_rows = out_0.rearrange("(p t) r -> p t r", t=PACK)
+        out_words = out_1[0].rearrange("p r t -> p (r t)").bitcast(I32)
+        starts = [sum(CHUNKS[:c]) for c in range(len(CHUNKS))]
+
+        def fetch(c):
+            n = CHUNKS[c]
+            entries = slice(starts[c] // 16, (starts[c] + n) // 16)
+            first = work.tile([P, PACK, n], F32, name="first", bufs=len(CHUNKS))
+            second = work.tile([P, PACK, n], F32, name="second", bufs=len(CHUNKS))
+            for t in range(PACK):
+                nc.scalar.activation(first[:, t, :], y_signed[t][:].indirect(t1_list[:, entries]), ACT.Copy)
+                nc.scalar.activation(second[:, t, :], y_scaled[t][:].indirect(t2_list[:, entries]), ACT.Copy)
+            return first, second
+
+        def hidden(c, first, second):
+            n = CHUNKS[c]
+            entries = slice(starts[c] // 16, (starts[c] + n) // 16)
+            larger = work.tile([P, PACK, n], F32, name="larger")
+            asked = work.tile([P, PACK, n], F32, name="asked", bufs=1, align_bytes=64)
+            for t in range(PACK):
+                nc.vector.scalar_tensor_tensor(
+                    larger[:, t, :], first[:, t, :], unit_tile[:, t : t + 1], second[:, t, :], ALU.mult, ALU.max
+                )
+            for t in range(PACK):
+                nc.vector.tensor_tensor(
+                    asked[:, t, :], ye_scaled[t][:].indirect(qw_list[:, entries]), larger[:, t, :], ALU.add
+                )
+            hid = work.tile([P, n * PACK], BF16, name="hid", align_bytes=64)
+            nc.vector.tensor_tensor(
+                hid[:].rearrange("p (c i t) -> p c t i", i=2, t=PACK),
+                asked[:].rearrange("p t (c i) -> p c t i", i=2),
+                first[:].rearrange("p t (c i) -> p c t i", i=2),
+                ALU.mult,
+            )
+            return hid
+
+        def answer(c, hid, w3_halves):
+            n = CHUNKS[c]
+            codes = work.tile([P, n], U32, name="hid_codes", align_bytes=64)
+            scales = work.tile([P, n], U8, name="hid_scales", align_bytes=64)
+            nc.vector.quantize_mx(out=codes[:].bitcast(FP8X4), scales=scales[:], in_=hid[:])
+            result = work.tile([P, PACK, n], F32, name="result", bufs=len(CHUNKS))
+            per_bank = min(PACK, 512 // n)
+            for t0 in range(0, PACK, per_bank):
+                bank = psum.tile([P, per_bank, n], F32, name="bank")
+                for t in range(t0, t0 + per_bank):
+                    product(bank[:, t - t0, :], w3_halves, t, codes[:], scales[:])
+                nc.scalar.copy(result[:, t0 : t0 + per_bank, :], bank[:])
+            nc.sync.dma_start(out_rows[:, :, starts[c] : starts[c] + n], result[:])
+            return result
+
+        def planes(c, result, copy):
+            n = CHUNKS[c]
+            cols = slice(starts[c], starts[c] + n)
+            rounded = keep.tile([P, n * PACK], BF16, name="rounded", tag=tags[c], align_bytes=64)
+            copy(
+                rounded[:].rearrange("p (c i t) -> p c t i", i=2, t=PACK),
+                result[:].rearrange("p t (c i) -> p c t i", i=2),
+            )
+            codes = work.tile([P, n], I32, name="out_codes", align_bytes=64, bufs=len(CHUNKS))
+            nc.vector.quantize_mx(out=codes[:].bitcast(FP8X4), scales=out_scales[:, cols], in_=rounded[:])
+            nc.sync.dma_start(out_words[:, cols], codes[:])
+
+        tags = ["y_signed%d" % t for t in range(PACK)] + ["y_scaled%d" % t for t in range(PACK)]
+        fetched = [fetch(c) for c in range(len(CHUNKS))]
+        w3_grouped = [round_weight_half(w3_raw, h, nc.vector.tensor_copy, "w3_grouped%d" % h) for h in range(2)]
+        w3_halves = [quantize_weight_half(w3_grouped[h], "w3_%d" % h) for h in range(2)]
+        results = []
+        last = len(CHUNKS) - 1
+        for c in range(len(CHUNKS)):
+            hid = hidden(c, *fetched[c])
+            results.append(answer(c, hid, w3_halves))
+        out_scales = work.tile([P, U], U8, name="out_scales", tag="asked", bufs=1, align_bytes=64)
+        for c in range(len(CHUNKS)):
+            planes(c, results[c], nc.vector.tensor_copy if c >= 3 else nc.scalar.copy)
+        for q in range(4):
+            queue = nc.sync if q % 2 == 0 else nc.scalar
+            queue.dma_start(out_2[0, 4 * q : 4 * q + 4, :].bitcast(I32), out_scales[32 * q : 32 * q + 4, :].bitcast(I32))

@@ -18,6 +18,7 @@ ACT = mybir.ActivationFunctionType
 P = 128
 PACK = 4
 CHUNKS = (256, 256, 256, 256)
+PIECE = 256
 
 
 def tile_picked_yvideoq_per_po_kernel(
@@ -38,6 +39,11 @@ def tile_picked_yvideoq_per_po_kernel(
         def load_weight(src, name):
             raw = keep.tile([P, PACK, N], F32, name=name)
             nc.sync.dma_start(raw[:], src.rearrange("(p j) n -> p j n", j=PACK))
+            return raw
+
+        def load_weight_columns(src, half, name):
+            raw = keep.tile([P, PACK, N // 2], F32, name=name)
+            nc.sync.dma_start(raw[:], src.rearrange("(p j) (h n) -> h p j n", j=PACK, h=2)[half])
             return raw
 
         def load_words(src, width, name):
@@ -85,12 +91,13 @@ def tile_picked_yvideoq_per_po_kernel(
             )
 
         offs_list = load_list(offs, "offs_list")
-        w1_raw = load_weight(w1, "w1_raw")
-        x_scale_table = load_scales(x_scales, T, "x_scale_table", nc.sync)
         unit_tile = keep.tile([P, PACK], F32, name="unit_tile")
         nc.sync.dma_start(unit_tile[:], unit.rearrange("(p t) o -> p (t o)", t=PACK))
-        wrd_list = load_list(wrd, "wrd_list")
         x_word_table = load_words(x_words, T, "x_word_table")
+        x_scale_table = load_scales(x_scales, T, "x_scale_table", nc.sync)
+        wrd_list = load_list(wrd, "wrd_list")
+        w1_left = load_weight_columns(w1, 0, "w1_left")
+        w1_right = load_weight_columns(w1, 1, "w1_right")
         e_word_table = load_words(e_words, W, "e_word_table")
         e_scale_table = load_scales(e_scales, W, "e_scale_table", nc.sync)
         t1_list = load_list(t1, "t1_list")
@@ -104,13 +111,17 @@ def tile_picked_yvideoq_per_po_kernel(
         nc.scalar.activation(unit_sign[:], unit_tile[:], ACT.Sign)
         nc.scalar.activation(unit_abs[:], unit_tile[:], ACT.Abs)
 
-        w1_grouped = [
-            round_weight_half(w1_raw, 0, nc.scalar.copy, "w1_grouped0"),
-            round_weight_half(w1_raw, 1, nc.scalar.copy, "w1_grouped1"),
-        ]
-        w1_halves = [quantize_weight_half(w1_grouped[h], "w1_%d" % h) for h in range(2)]
         x_codes = pick(x_word_table[:].bitcast(U32), offs_list, U32, "x_codes")
         x_bytes = pick(x_scale_table[:], offs_list, U8, "x_bytes")
+        w1_grouped = [keep.tile([P, 2 * P * PACK], BF16, name="w1_grouped%d" % h, align_bytes=64) for h in range(2)]
+        for side, raw in enumerate((w1_left, w1_right)):
+            for half in range(2):
+                copy = nc.vector.tensor_copy if (side, half) == (1, 0) else nc.scalar.copy
+                copy(
+                    w1_grouped[half][:].rearrange("p (e s m j) -> p s m j e", e=2, s=2, j=PACK)[:, side],
+                    raw[:].rearrange("p j (m u e) -> p u m j e", u=2, e=2)[:, half],
+                )
+        w1_halves = [quantize_weight_half(w1_grouped[h], "w1_%d" % h) for h in range(2)]
         y_signed, y_scaled, ye_scaled = [], [], []
         for t in range(PACK):
             bank = psum.tile([P, S], F32, name="bank")
@@ -120,15 +131,15 @@ def tile_picked_yvideoq_per_po_kernel(
             y_scaled.append(keep.tile([P, S], F32, name="y_scaled%d" % t, align_bytes=64))
             nc.vector.tensor_scalar(y_scaled[t][:], y_signed[t][:], unit_tile[:, t : t + 1], None, ALU.mult)
 
-        e_bytes = pick(e_scale_table[:], wrd_list, U8, "e_bytes")
         e_codes = pick(e_word_table[:].bitcast(U32), wrd_list, U32, "e_codes")
+        e_bytes = pick(e_scale_table[:], wrd_list, U8, "e_bytes")
         w2_grouped = [round_weight_half(w2_raw, h, nc.vector.tensor_copy, "w2_grouped%d" % h) for h in range(2)]
         w2_halves = [quantize_weight_half(w2_grouped[h], "w2_%d" % h) for h in range(2)]
         for t in range(PACK):
             bank = psum.tile([P, S], F32, name="bank")
             product(bank[:], w2_halves, t, e_codes[:], e_bytes[:])
             ye_scaled.append(keep.tile([P, S], F32, name="ye_scaled%d" % t, align_bytes=64))
-            if t < 2:
+            if t not in (0, 1):
                 nc.vector.tensor_scalar(ye_scaled[t][:], bank[:], unit_abs[:, t : t + 1], None, ALU.mult)
             else:
                 nc.scalar.activation(ye_scaled[t][:], bank[:], ACT.Copy, scale=unit_abs[:, t : t + 1])
@@ -136,12 +147,26 @@ def tile_picked_yvideoq_per_po_kernel(
         out_rows = out_0.rearrange("(p t) r -> p t r", t=PACK)
         out_words = out_1[0].rearrange("p r t -> p (r t)").bitcast(I32)
         starts = [sum(CHUNKS[:c]) for c in range(len(CHUNKS))]
+        last = len(CHUNKS) - 1
+
+        held = 1
+        early = starts[held]
+        firsts = [
+            keep.tile([P, PACK * early], F32, name="first_early", align_bytes=64),
+            keep.tile([P, PACK * (U - early)], F32, name="first_late", tag="w2_1_codes", align_bytes=64),
+        ]
+        seconds = [
+            keep.tile([P, PACK * early], F32, name="second_early", align_bytes=64),
+            keep.tile([P, PACK * (U - early)], F32, name="second_late", tag="w2_1_scales", align_bytes=64),
+        ]
 
         def fetch(c):
             n = CHUNKS[c]
             entries = slice(starts[c] // 16, (starts[c] + n) // 16)
-            first = work.tile([P, PACK, n], F32, name="first", bufs=len(CHUNKS))
-            second = work.tile([P, PACK, n], F32, name="second", bufs=len(CHUNKS))
+            late = int(c >= held)
+            lo = PACK * (starts[c] - late * early)
+            first = firsts[late][:, lo : lo + PACK * n].rearrange("p (t r) -> p t r", t=PACK)
+            second = seconds[late][:, lo : lo + PACK * n].rearrange("p (t r) -> p t r", t=PACK)
             for t in range(PACK):
                 nc.scalar.activation(first[:, t, :], y_signed[t][:].indirect(t1_list[:, entries]), ACT.Copy)
                 nc.scalar.activation(second[:, t, :], y_scaled[t][:].indirect(t2_list[:, entries]), ACT.Copy)
@@ -160,54 +185,61 @@ def tile_picked_yvideoq_per_po_kernel(
                 nc.vector.tensor_tensor(
                     asked[:, t, :], ye_scaled[t][:].indirect(qw_list[:, entries]), larger[:, t, :], ALU.add
                 )
-            hid = work.tile([P, n * PACK], BF16, name="hid", align_bytes=64)
+            return asked
+
+        def answer(start, width, asked, first, w3_halves):
+            hid = work.tile([P, width * PACK], BF16, name="hid", align_bytes=64)
             nc.vector.tensor_tensor(
                 hid[:].rearrange("p (c i t) -> p c t i", i=2, t=PACK),
-                asked[:].rearrange("p t (c i) -> p c t i", i=2),
-                first[:].rearrange("p t (c i) -> p c t i", i=2),
+                asked.rearrange("p t (c i) -> p c t i", i=2),
+                first.rearrange("p t (c i) -> p c t i", i=2),
                 ALU.mult,
             )
-            return hid
-
-        def answer(c, hid, w3_halves):
-            n = CHUNKS[c]
-            codes = work.tile([P, n], U32, name="hid_codes", align_bytes=64)
-            scales = work.tile([P, n], U8, name="hid_scales", align_bytes=64)
+            codes = keep.tile([P, width], U32, name="hid_codes%d" % start, align_bytes=64)
+            scales = keep.tile([P, width], U8, name="hid_scales%d" % start, align_bytes=64)
             nc.vector.quantize_mx(out=codes[:].bitcast(FP8X4), scales=scales[:], in_=hid[:])
-            result = work.tile([P, PACK, n], F32, name="result", bufs=len(CHUNKS))
-            per_bank = min(PACK, 512 // n)
+            result = keep.tile([P, PACK, width], F32, name="result%d" % start)
+            per_bank = 512 // width
             for t0 in range(0, PACK, per_bank):
-                bank = psum.tile([P, per_bank, n], F32, name="bank")
+                bank = psum.tile([P, per_bank, width], F32, name="bank")
                 for t in range(t0, t0 + per_bank):
                     product(bank[:, t - t0, :], w3_halves, t, codes[:], scales[:])
                 nc.scalar.copy(result[:, t0 : t0 + per_bank, :], bank[:])
-            nc.sync.dma_start(out_rows[:, :, starts[c] : starts[c] + n], result[:])
-            return result
+                nc.sync.dma_start(out_rows[:, t0 : t0 + per_bank, start : start + width], result[:, t0 : t0 + per_bank, :])
 
-        def planes(c, result, copy):
-            n = CHUNKS[c]
-            cols = slice(starts[c], starts[c] + n)
-            rounded = keep.tile([P, n * PACK], BF16, name="rounded", tag=tags[c], align_bytes=64)
+            return start, width, result
+
+        def planes(start, width, result, copy, tag):
+            cols = slice(start, start + width)
+            rounded = keep.tile([P, width * PACK], BF16, name="rounded", tag=tag, align_bytes=64)
             copy(
                 rounded[:].rearrange("p (c i t) -> p c t i", i=2, t=PACK),
                 result[:].rearrange("p t (c i) -> p c t i", i=2),
             )
-            codes = work.tile([P, n], I32, name="out_codes", align_bytes=64, bufs=len(CHUNKS))
-            nc.vector.quantize_mx(out=codes[:].bitcast(FP8X4), scales=out_scales[:, cols], in_=rounded[:])
-            nc.sync.dma_start(out_words[:, cols], codes[:])
+            nc.vector.quantize_mx(out=out_codes[:, cols].bitcast(FP8X4), scales=out_scales[:, cols], in_=rounded[:])
+            if start + width in (starts[last], U):
+                stored = slice(0 if start < starts[last] else starts[last], start + width)
+                nc.sync.dma_start(out_words[:, stored], out_codes[:, stored])
 
-        tags = ["y_signed%d" % t for t in range(PACK)] + ["y_scaled%d" % t for t in range(PACK)]
         fetched = [fetch(c) for c in range(len(CHUNKS))]
         w3_grouped = [round_weight_half(w3_raw, h, nc.vector.tensor_copy, "w3_grouped%d" % h) for h in range(2)]
         w3_halves = [quantize_weight_half(w3_grouped[h], "w3_%d" % h) for h in range(2)]
-        results = []
-        last = len(CHUNKS) - 1
+        pieces = []
         for c in range(len(CHUNKS)):
-            hid = hidden(c, *fetched[c])
-            results.append(answer(c, hid, w3_halves))
+            asked = hidden(c, *fetched[c])
+            width = 256 if c == last else CHUNKS[c]
+            for lo in range(0, CHUNKS[c], width):
+                cols = slice(lo, lo + width)
+                pieces.append(answer(starts[c] + lo, width, asked[:, :, cols], fetched[c][0][:, :, cols], w3_halves))
         out_scales = work.tile([P, U], U8, name="out_scales", tag="asked", bufs=1, align_bytes=64)
-        for c in range(len(CHUNKS)):
-            planes(c, results[c], nc.vector.tensor_copy if c >= 3 else nc.scalar.copy)
+        out_codes = keep.tile([P, U], I32, name="out_codes", align_bytes=64)
+        s_tags = ["hid_codes512", "hid_scales512", "y_signed0"]
+        v_tags = ["w2_1_codes", "w2_1_scales", "ye_scaled3", "ye_scaled2", "ye_scaled1", "ye_scaled0"]
+        for i, (start, width, result) in enumerate(pieces):
+            if i < 2:
+                planes(start, width, result, nc.scalar.copy, s_tags[i])
+            else:
+                planes(start, width, result, nc.vector.tensor_copy, v_tags[i % 2])
         for q in range(4):
             queue = nc.sync if q % 2 == 0 else nc.scalar
             queue.dma_start(out_2[0, 4 * q : 4 * q + 4, :].bitcast(I32), out_scales[32 * q : 32 * q + 4, :].bitcast(I32))

@@ -17,8 +17,17 @@ ACT = mybir.ActivationFunctionType
 
 P = 128
 PACK = 4
-CHUNKS = (256, 256, 256, 256)
-PIECE = 256
+QUADRANT = 32
+LIST_ROWS = 16
+BANK = 512
+CHUNK = 256
+CHUNKS = U // CHUNK
+LAST = CHUNKS - 1
+TAIL_PIECE = 128
+
+YE_PLANES_ON_SCALAR = 3
+QW_PLANES_ON_SCALAR = 1
+ROUNDED_ON_SCALAR = 2
 
 
 def tile_picked_yvideoq_per_po_kernel(
@@ -37,13 +46,8 @@ def tile_picked_yvideoq_per_po_kernel(
             return tile
 
         def load_weight(src, name):
-            raw = keep.tile([P, PACK, N], F32, name=name)
+            raw = keep.tile([P, PACK, src.shape[1]], F32, name=name)
             nc.sync.dma_start(raw[:], src.rearrange("(p j) n -> p j n", j=PACK))
-            return raw
-
-        def load_weight_columns(src, half, name):
-            raw = keep.tile([P, PACK, N // 2], F32, name=name)
-            nc.sync.dma_start(raw[:], src.rearrange("(p j) (h n) -> h p j n", j=PACK, h=2)[half])
             return raw
 
         def load_words(src, width, name):
@@ -51,11 +55,11 @@ def tile_picked_yvideoq_per_po_kernel(
             nc.sync.dma_start(table[:], src[0].rearrange("p n t -> p (n t)").bitcast(I32))
             return table
 
-        def load_scales(src, width, name, queue):
+        def load_scales(src, width, name):
             table = keep.tile([P, width], U8, name=name)
             nc.vector.memset(table[:].bitcast(I32), 0)
-            for q in range(4):
-                queue.dma_start(table[32 * q : 32 * q + 4, :].bitcast(I32), src[0, 4 * q : 4 * q + 4, :].bitcast(I32))
+            for r in range(PACK):
+                nc.sync.dma_start(table[r:P:QUADRANT, :].bitcast(I32), src[0, r::PACK, :].bitcast(I32))
             return table
 
         def pick(table_view, offsets, dtype, name):
@@ -63,22 +67,22 @@ def tile_picked_yvideoq_per_po_kernel(
             nc.vector.tensor_copy(picked[:], table_view.indirect(offsets[:]))
             return picked
 
-        def round_weight_half(raw, half, copy, name):
+        def round_weight_pair(raw, pair, name):
             grouped = keep.tile([P, 2 * P * PACK], BF16, name=name, align_bytes=64)
-            copy(
+            nc.vector.tensor_copy(
                 grouped[:].rearrange("p (e m j) -> p m j e", e=2, j=PACK),
-                raw[:].rearrange("p j (m u e) -> p u m j e", u=2, e=2)[:, half],
+                raw[:].rearrange("p j (m u e) -> p u m j e", u=2, e=2)[:, pair],
             )
             return grouped
 
-        def quantize_weight_half(grouped, name):
+        def quantize_weight_pair(grouped, name):
             codes = keep.tile([P, 2 * P], U32, name=name + "_codes", align_bytes=64)
             scales = keep.tile([P, 2 * P], U8, name=name + "_scales", align_bytes=64)
             nc.vector.quantize_mx(out=codes[:].bitcast(FP8X4), scales=scales[:], in_=grouped[:])
             return codes, scales
 
-        def product(out, halves, t, codes, scales):
-            w_codes, w_scales = halves[t // 2]
+        def product(out, w_pairs, t, codes, scales):
+            w_codes, w_scales = w_pairs[t // 2]
             cols = slice((t % 2) * P, (t % 2 + 1) * P)
             nc.tensor.matmul_mx(
                 out=out,
@@ -90,16 +94,25 @@ def tile_picked_yvideoq_per_po_kernel(
                 stop=True,
             )
 
+        def interleaved(tile):
+            return tile[:].rearrange("p (c i t) -> p c t i", i=2, t=PACK)
+
+        def planes_walk(planes):
+            return planes.rearrange("p t (c i) -> p c t i", i=2)
+
+        def entries(c):
+            return slice(c * CHUNK // LIST_ROWS, (c + 1) * CHUNK // LIST_ROWS)
+
         offs_list = load_list(offs, "offs_list")
         unit_tile = keep.tile([P, PACK], F32, name="unit_tile")
         nc.sync.dma_start(unit_tile[:], unit.rearrange("(p t) o -> p (t o)", t=PACK))
         x_word_table = load_words(x_words, T, "x_word_table")
-        x_scale_table = load_scales(x_scales, T, "x_scale_table", nc.sync)
+        x_scale_table = load_scales(x_scales, T, "x_scale_table")
         wrd_list = load_list(wrd, "wrd_list")
-        w1_left = load_weight_columns(w1, 0, "w1_left")
-        w1_right = load_weight_columns(w1, 1, "w1_right")
+        w1_left = load_weight(w1[:, : N // 2], "w1_left")
+        w1_right = load_weight(w1[:, N // 2 :], "w1_right")
         e_word_table = load_words(e_words, W, "e_word_table")
-        e_scale_table = load_scales(e_scales, W, "e_scale_table", nc.sync)
+        e_scale_table = load_scales(e_scales, W, "e_scale_table")
         t1_list = load_list(t1, "t1_list")
         w2_raw = load_weight(w2, "w2_raw")
         t2_list = load_list(t2, "t2_list")
@@ -113,19 +126,19 @@ def tile_picked_yvideoq_per_po_kernel(
 
         x_codes = pick(x_word_table[:].bitcast(U32), offs_list, U32, "x_codes")
         x_bytes = pick(x_scale_table[:], offs_list, U8, "x_bytes")
-        w1_grouped = [keep.tile([P, 2 * P * PACK], BF16, name="w1_grouped%d" % h, align_bytes=64) for h in range(2)]
+        w1_grouped = [keep.tile([P, 2 * P * PACK], BF16, name="w1_grouped%d" % u, align_bytes=64) for u in range(2)]
+        w1_copies = ((nc.scalar.copy, nc.scalar.copy), (nc.vector.tensor_copy, nc.scalar.copy))
         for side, raw in enumerate((w1_left, w1_right)):
-            for half in range(2):
-                copy = nc.vector.tensor_copy if (side, half) == (1, 0) else nc.scalar.copy
-                copy(
-                    w1_grouped[half][:].rearrange("p (e s m j) -> p s m j e", e=2, s=2, j=PACK)[:, side],
-                    raw[:].rearrange("p j (m u e) -> p u m j e", u=2, e=2)[:, half],
+            for pair in range(2):
+                w1_copies[side][pair](
+                    w1_grouped[pair][:].rearrange("p (e s m j) -> p s m j e", e=2, s=2, j=PACK)[:, side],
+                    raw[:].rearrange("p j (m u e) -> p u m j e", u=2, e=2)[:, pair],
                 )
-        w1_halves = [quantize_weight_half(w1_grouped[h], "w1_%d" % h) for h in range(2)]
+        w1_pairs = [quantize_weight_pair(w1_grouped[u], "w1_%d" % u) for u in range(2)]
         y_signed, y_scaled, ye_scaled = [], [], []
         for t in range(PACK):
             bank = psum.tile([P, S], F32, name="bank")
-            product(bank[:], w1_halves, t, x_codes[:], x_bytes[:])
+            product(bank[:], w1_pairs, t, x_codes[:], x_bytes[:])
             y_signed.append(keep.tile([P, S], F32, name="y_signed%d" % t, align_bytes=64))
             nc.scalar.activation(y_signed[t][:], bank[:], ACT.Copy, scale=unit_sign[:, t : t + 1])
             y_scaled.append(keep.tile([P, S], F32, name="y_scaled%d" % t, align_bytes=64))
@@ -133,113 +146,103 @@ def tile_picked_yvideoq_per_po_kernel(
 
         e_codes = pick(e_word_table[:].bitcast(U32), wrd_list, U32, "e_codes")
         e_bytes = pick(e_scale_table[:], wrd_list, U8, "e_bytes")
-        w2_grouped = [round_weight_half(w2_raw, h, nc.vector.tensor_copy, "w2_grouped%d" % h) for h in range(2)]
-        w2_halves = [quantize_weight_half(w2_grouped[h], "w2_%d" % h) for h in range(2)]
+        w2_grouped = [round_weight_pair(w2_raw, u, "w2_grouped%d" % u) for u in range(2)]
+        w2_pairs = [quantize_weight_pair(w2_grouped[u], "w2_%d" % u) for u in range(2)]
         for t in range(PACK):
             bank = psum.tile([P, S], F32, name="bank")
-            product(bank[:], w2_halves, t, e_codes[:], e_bytes[:])
+            product(bank[:], w2_pairs, t, e_codes[:], e_bytes[:])
             ye_scaled.append(keep.tile([P, S], F32, name="ye_scaled%d" % t, align_bytes=64))
-            if t not in (0, 1):
-                nc.vector.tensor_scalar(ye_scaled[t][:], bank[:], unit_abs[:, t : t + 1], None, ALU.mult)
-            else:
+            if t < YE_PLANES_ON_SCALAR:
                 nc.scalar.activation(ye_scaled[t][:], bank[:], ACT.Copy, scale=unit_abs[:, t : t + 1])
+            else:
+                nc.vector.tensor_scalar(ye_scaled[t][:], bank[:], unit_abs[:, t : t + 1], None, ALU.mult)
+
+        later_first_tag, later_second_tag = "w2_1_codes", "w2_1_scales"
+        first_early = keep.tile([P, PACK * CHUNK], F32, name="first_early", align_bytes=64)
+        first_later = keep.tile([P, PACK * CHUNK * LAST], F32, name="first_later", tag=later_first_tag, align_bytes=64)
+        second_early = keep.tile([P, PACK * CHUNK], F32, name="second_early", align_bytes=64)
+        second_later = keep.tile([P, PACK * CHUNK * LAST], F32, name="second_later", tag=later_second_tag, align_bytes=64)
+
+        def chunk_planes(early, later, c):
+            flat = early[:] if c == 0 else later[:, PACK * CHUNK * (c - 1) : PACK * CHUNK * c]
+            return flat.rearrange("p (t r) -> p t r", t=PACK)
+
+        firsts = [chunk_planes(first_early, first_later, c) for c in range(CHUNKS)]
+        seconds = [chunk_planes(second_early, second_later, c) for c in range(CHUNKS)]
+        for c in range(CHUNKS):
+            for t in range(PACK):
+                nc.scalar.activation(firsts[c][:, t, :], y_signed[t][:].indirect(t1_list[:, entries(c)]), ACT.Copy)
+                nc.scalar.activation(seconds[c][:, t, :], y_scaled[t][:].indirect(t2_list[:, entries(c)]), ACT.Copy)
+        last_fused = PACK - QW_PLANES_ON_SCALAR
+        last_eq = keep.tile([P, QW_PLANES_ON_SCALAR, CHUNK], F32, name="last_eq")
+        for t in range(last_fused, PACK):
+            nc.scalar.activation(last_eq[:, t - last_fused, :], ye_scaled[t][:].indirect(qw_list[:, entries(LAST)]), ACT.Copy)
+
+        w3_grouped = [round_weight_pair(w3_raw, u, "w3_grouped%d" % u) for u in range(2)]
+        w3_pairs = [quantize_weight_pair(w3_grouped[u], "w3_%d" % u) for u in range(2)]
+
+        def scaled_fq(c):
+            larger = work.tile([P, PACK, CHUNK], F32, name="larger")
+            fq = work.tile([P, PACK, CHUNK], F32, name="fq", bufs=1, align_bytes=64)
+            for t in range(PACK):
+                nc.vector.scalar_tensor_tensor(
+                    larger[:, t, :], firsts[c][:, t, :], unit_tile[:, t : t + 1], seconds[c][:, t, :], ALU.mult, ALU.max
+                )
+            fused = last_fused if c == LAST else PACK
+            for t in range(fused):
+                nc.vector.tensor_tensor(
+                    fq[:, t, :], ye_scaled[t][:].indirect(qw_list[:, entries(c)]), larger[:, t, :], ALU.add
+                )
+            if c == LAST:
+                nc.vector.tensor_tensor(fq[:, fused:, :], last_eq[:], larger[:, fused:, :], ALU.add)
+            return fq
 
         out_rows = out_0.rearrange("(p t) r -> p t r", t=PACK)
         out_words = out_1[0].rearrange("p r t -> p (r t)").bitcast(I32)
-        starts = [sum(CHUNKS[:c]) for c in range(len(CHUNKS))]
-        last = len(CHUNKS) - 1
 
-        held = 1
-        early = starts[held]
-        firsts = [
-            keep.tile([P, PACK * early], F32, name="first_early", align_bytes=64),
-            keep.tile([P, PACK * (U - early)], F32, name="first_late", tag="w2_1_codes", align_bytes=64),
-        ]
-        seconds = [
-            keep.tile([P, PACK * early], F32, name="second_early", align_bytes=64),
-            keep.tile([P, PACK * (U - early)], F32, name="second_late", tag="w2_1_scales", align_bytes=64),
-        ]
-
-        def fetch(c):
-            n = CHUNKS[c]
-            entries = slice(starts[c] // 16, (starts[c] + n) // 16)
-            late = int(c >= held)
-            lo = PACK * (starts[c] - late * early)
-            first = firsts[late][:, lo : lo + PACK * n].rearrange("p (t r) -> p t r", t=PACK)
-            second = seconds[late][:, lo : lo + PACK * n].rearrange("p (t r) -> p t r", t=PACK)
-            for t in range(PACK):
-                nc.scalar.activation(first[:, t, :], y_signed[t][:].indirect(t1_list[:, entries]), ACT.Copy)
-                nc.scalar.activation(second[:, t, :], y_scaled[t][:].indirect(t2_list[:, entries]), ACT.Copy)
-            return first, second
-
-        def hidden(c, first, second):
-            n = CHUNKS[c]
-            entries = slice(starts[c] // 16, (starts[c] + n) // 16)
-            larger = work.tile([P, PACK, n], F32, name="larger")
-            asked = work.tile([P, PACK, n], F32, name="asked", bufs=1, align_bytes=64)
-            for t in range(PACK):
-                nc.vector.scalar_tensor_tensor(
-                    larger[:, t, :], first[:, t, :], unit_tile[:, t : t + 1], second[:, t, :], ALU.mult, ALU.max
-                )
-            for t in range(PACK):
-                nc.vector.tensor_tensor(
-                    asked[:, t, :], ye_scaled[t][:].indirect(qw_list[:, entries]), larger[:, t, :], ALU.add
-                )
-            return asked
-
-        def answer(start, width, asked, first, w3_halves):
+        def answer(start, width, fq, first):
             hid = work.tile([P, width * PACK], BF16, name="hid", align_bytes=64)
-            nc.vector.tensor_tensor(
-                hid[:].rearrange("p (c i t) -> p c t i", i=2, t=PACK),
-                asked.rearrange("p t (c i) -> p c t i", i=2),
-                first.rearrange("p t (c i) -> p c t i", i=2),
-                ALU.mult,
-            )
+            nc.vector.tensor_tensor(interleaved(hid), planes_walk(fq), planes_walk(first), ALU.mult)
             codes = keep.tile([P, width], U32, name="hid_codes%d" % start, align_bytes=64)
             scales = keep.tile([P, width], U8, name="hid_scales%d" % start, align_bytes=64)
             nc.vector.quantize_mx(out=codes[:].bitcast(FP8X4), scales=scales[:], in_=hid[:])
             result = keep.tile([P, PACK, width], F32, name="result%d" % start)
-            per_bank = 512 // width
+            per_bank = BANK // width
             for t0 in range(0, PACK, per_bank):
                 bank = psum.tile([P, per_bank, width], F32, name="bank")
                 for t in range(t0, t0 + per_bank):
-                    product(bank[:, t - t0, :], w3_halves, t, codes[:], scales[:])
-                nc.scalar.copy(result[:, t0 : t0 + per_bank, :], bank[:])
-                nc.sync.dma_start(out_rows[:, t0 : t0 + per_bank, start : start + width], result[:, t0 : t0 + per_bank, :])
-
+                    product(bank[:, t - t0, :], w3_pairs, t, codes[:], scales[:])
+                held = slice(t0, t0 + per_bank)
+                nc.scalar.copy(result[:, held, :], bank[:])
+                nc.sync.dma_start(out_rows[:, held, start : start + width], result[:, held, :])
             return start, width, result
 
-        def planes(start, width, result, copy, tag):
-            cols = slice(start, start + width)
-            rounded = keep.tile([P, width * PACK], BF16, name="rounded", tag=tag, align_bytes=64)
-            copy(
-                rounded[:].rearrange("p (c i t) -> p c t i", i=2, t=PACK),
-                result[:].rearrange("p t (c i) -> p c t i", i=2),
-            )
-            nc.vector.quantize_mx(out=out_codes[:, cols].bitcast(FP8X4), scales=out_scales[:, cols], in_=rounded[:])
-            if start + width in (starts[last], U):
-                stored = slice(0 if start < starts[last] else starts[last], start + width)
-                nc.sync.dma_start(out_words[:, stored], out_codes[:, stored])
-
-        fetched = [fetch(c) for c in range(len(CHUNKS))]
-        w3_grouped = [round_weight_half(w3_raw, h, nc.vector.tensor_copy, "w3_grouped%d" % h) for h in range(2)]
-        w3_halves = [quantize_weight_half(w3_grouped[h], "w3_%d" % h) for h in range(2)]
         pieces = []
-        for c in range(len(CHUNKS)):
-            asked = hidden(c, *fetched[c])
-            width = 256 if c == last else CHUNKS[c]
-            for lo in range(0, CHUNKS[c], width):
+        for c in range(CHUNKS):
+            fq = scaled_fq(c)
+            width = TAIL_PIECE if c == LAST else CHUNK
+            for lo in range(0, CHUNK, width):
                 cols = slice(lo, lo + width)
-                pieces.append(answer(starts[c] + lo, width, asked[:, :, cols], fetched[c][0][:, :, cols], w3_halves))
-        out_scales = work.tile([P, U], U8, name="out_scales", tag="asked", bufs=1, align_bytes=64)
+                pieces.append(answer(c * CHUNK + lo, width, fq[:, :, cols], firsts[c][:, :, cols]))
+
+        out_scales = work.tile([P, U], U8, name="out_scales", tag="fq", bufs=1, align_bytes=64)
         out_codes = keep.tile([P, U], I32, name="out_codes", align_bytes=64)
-        s_tags = ["hid_codes512", "hid_scales512", "y_signed0"]
-        v_tags = ["w2_1_codes", "w2_1_scales", "ye_scaled3", "ye_scaled2", "ye_scaled1", "ye_scaled0"]
+        last_start = LAST * CHUNK
+        scalar_tags = ("hid_codes%d" % (last_start - CHUNK), "hid_scales%d" % (last_start - CHUNK))
+        vector_tags = (later_first_tag, later_second_tag)
         for i, (start, width, result) in enumerate(pieces):
-            if i < 2:
-                planes(start, width, result, nc.scalar.copy, s_tags[i])
+            if i < ROUNDED_ON_SCALAR:
+                copy, tag = nc.scalar.copy, scalar_tags[i]
             else:
-                planes(start, width, result, nc.vector.tensor_copy, v_tags[i % 2])
-        for q in range(4):
-            queue = nc.sync if q % 2 == 0 else nc.scalar
-            queue.dma_start(out_2[0, 4 * q : 4 * q + 4, :].bitcast(I32), out_scales[32 * q : 32 * q + 4, :].bitcast(I32))
+                copy, tag = nc.vector.tensor_copy, vector_tags[i % 2]
+            rounded = keep.tile([P, width * PACK], BF16, name="rounded", tag=tag, align_bytes=64)
+            copy(interleaved(rounded), planes_walk(result[:]))
+            cols = slice(start, start + width)
+            nc.vector.quantize_mx(out=out_codes[:, cols].bitcast(FP8X4), scales=out_scales[:, cols], in_=rounded[:])
+            if start + width == last_start:
+                nc.sync.dma_start(out_words[:, :last_start], out_codes[:, :last_start])
+            elif start + width == U:
+                nc.sync.dma_start(out_words[:, last_start:], out_codes[:, last_start:])
+        for r in range(PACK):
+            queue = nc.sync if r % 2 == 0 else nc.scalar
+            queue.dma_start(out_2[0, r::PACK, :].bitcast(I32), out_scales[r:P:QUADRANT, :].bitcast(I32))

from contextlib import ExitStack

import concourse.mybir as mybir

K, T, S, N, H, W, U = 512, 2048, 512, 512, 512, 1024, 1024
FLOPS = 2 * K * N * S * 2 + 2 * H * N * U

F32 = mybir.dt.float32
BF16 = mybir.dt.bfloat16
I32 = mybir.dt.int32
U32 = mybir.dt.uint32
U16 = mybir.dt.uint16
U8 = mybir.dt.uint8
FP8X4 = mybir.dt.float8_e4m3fn_x4
ALU = mybir.AluOpType
ACT = mybir.ActivationFunctionType

P = 128
PACK = 4
QUADRANT = 32
LIST_ROWS = 16
BANK = 512
CHUNK = 256
CHUNKS = U // CHUNK
LAST = CHUNKS - 1
TAIL_PIECE = 128

YE_PLANES_ON_SCALAR = 3
QW_PLANES_ON_SCALAR = 1
ROUNDED_ON_SCALAR = 2


def tile_picked_yvideoq_per_po_kernel(
    tc, x_words, x_scales, w1, e_words, e_scales, w2, unit, w3, offs, wrd, t1, t2, qw, out_0, out_1, out_2
):
    nc = tc.nc
    with ExitStack() as ctx:
        lists = ctx.enter_context(tc.tile_pool(name="lists", bufs=1))
        keep = ctx.enter_context(tc.tile_pool(name="keep", bufs=1))
        work = ctx.enter_context(tc.tile_pool(name="work", bufs=2))
        psum = ctx.enter_context(tc.psum_pool(name="psum", bufs=8))

        def load_list(src, name):
            tile = lists.tile(list(src.shape), U16, name=name)
            nc.sync.dma_start(tile[:], src)
            return tile

        def load_weight(src, name):
            raw = keep.tile([P, PACK, src.shape[1]], F32, name=name)
            nc.sync.dma_start(raw[:], src.rearrange("(p j) n -> p j n", j=PACK))
            return raw

        def load_words(src, width, name):
            table = keep.tile([P, width], I32, name=name)
            nc.sync.dma_start(table[:], src[0].rearrange("p n t -> p (n t)").bitcast(I32))
            return table

        def load_scales(src, width, name):
            table = keep.tile([P, width], U8, name=name)
            nc.vector.memset(table[:].bitcast(I32), 0)
            for r in range(PACK):
                nc.sync.dma_start(table[r:P:QUADRANT, :].bitcast(I32), src[0, r::PACK, :].bitcast(I32))
            return table

        def pick(table_view, offsets, dtype, name):
            picked = keep.tile([P, S], dtype, name=name, align_bytes=64)
            nc.vector.tensor_copy(picked[:], table_view.indirect(offsets[:]))
            return picked

        def round_weight_pair(raw, pair, name):
            grouped = keep.tile([P, 2 * P * PACK], BF16, name=name, align_bytes=64)
            nc.vector.tensor_copy(
                grouped[:].rearrange("p (e m j) -> p m j e", e=2, j=PACK),
                raw[:].rearrange("p j (m u e) -> p u m j e", u=2, e=2)[:, pair],
            )
            return grouped

        def quantize_weight_pair(grouped, name):
            codes = keep.tile([P, 2 * P], U32, name=name + "_codes", align_bytes=64)
            scales = keep.tile([P, 2 * P], U8, name=name + "_scales", align_bytes=64)
            nc.vector.quantize_mx(out=codes[:].bitcast(FP8X4), scales=scales[:], in_=grouped[:])
            return codes, scales

        def product(out, w_pairs, t, codes, scales):
            w_codes, w_scales = w_pairs[t // 2]
            cols = slice((t % 2) * P, (t % 2 + 1) * P)
            nc.tensor.matmul_mx(
                out=out,
                lhsT=w_codes[:, cols].bitcast(FP8X4),
                lhsT_scale=w_scales[:, cols],
                rhs=codes.bitcast(FP8X4),
                rhs_scale=scales,
                start=True,
                stop=True,
            )

        def interleaved(tile):
            return tile[:].rearrange("p (c i t) -> p c t i", i=2, t=PACK)

        def planes_walk(planes):
            return planes.rearrange("p t (c i) -> p c t i", i=2)

        def entries(c):
            return slice(c * CHUNK // LIST_ROWS, (c + 1) * CHUNK // LIST_ROWS)

        offs_list = load_list(offs, "offs_list")
        unit_tile = keep.tile([P, PACK], F32, name="unit_tile")
        nc.sync.dma_start(unit_tile[:], unit.rearrange("(p t) o -> p (t o)", t=PACK))
        x_word_table = load_words(x_words, T, "x_word_table")
        x_scale_table = load_scales(x_scales, T, "x_scale_table")
        wrd_list = load_list(wrd, "wrd_list")
        w1_left = load_weight(w1[:, : N // 2], "w1_left")
        w1_right = load_weight(w1[:, N // 2 :], "w1_right")
        e_word_table = load_words(e_words, W, "e_word_table")
        e_scale_table = load_scales(e_scales, W, "e_scale_table")
        t1_list = load_list(t1, "t1_list")
        w2_raw = load_weight(w2, "w2_raw")
        t2_list = load_list(t2, "t2_list")
        qw_list = load_list(qw, "qw_list")
        w3_raw = load_weight(w3, "w3_raw")

        unit_sign = keep.tile([P, PACK], F32, name="unit_sign")
        unit_abs = keep.tile([P, PACK], F32, name="unit_abs")
        nc.scalar.activation(unit_sign[:], unit_tile[:], ACT.Sign)
        nc.scalar.activation(unit_abs[:], unit_tile[:], ACT.Abs)

        x_codes = pick(x_word_table[:].bitcast(U32), offs_list, U32, "x_codes")
        x_bytes = pick(x_scale_table[:], offs_list, U8, "x_bytes")
        w1_grouped = [keep.tile([P, 2 * P * PACK], BF16, name="w1_grouped%d" % u, align_bytes=64) for u in range(2)]
        w1_copies = ((nc.scalar.copy, nc.scalar.copy), (nc.vector.tensor_copy, nc.scalar.copy))
        for side, raw in enumerate((w1_left, w1_right)):
            for pair in range(2):
                w1_copies[side][pair](
                    w1_grouped[pair][:].rearrange("p (e s m j) -> p s m j e", e=2, s=2, j=PACK)[:, side],
                    raw[:].rearrange("p j (m u e) -> p u m j e", u=2, e=2)[:, pair],
                )
        w1_pairs = [quantize_weight_pair(w1_grouped[u], "w1_%d" % u) for u in range(2)]
        y_signed, y_scaled, ye_scaled = [], [], []
        for t in range(PACK):
            bank = psum.tile([P, S], F32, name="bank")
            product(bank[:], w1_pairs, t, x_codes[:], x_bytes[:])
            y_signed.append(keep.tile([P, S], F32, name="y_signed%d" % t, align_bytes=64))
            nc.scalar.activation(y_signed[t][:], bank[:], ACT.Copy, scale=unit_sign[:, t : t + 1])
            y_scaled.append(keep.tile([P, S], F32, name="y_scaled%d" % t, align_bytes=64))
            nc.vector.tensor_scalar(y_scaled[t][:], y_signed[t][:], unit_tile[:, t : t + 1], None, ALU.mult)

        e_codes = pick(e_word_table[:].bitcast(U32), wrd_list, U32, "e_codes")
        e_bytes = pick(e_scale_table[:], wrd_list, U8, "e_bytes")
        w2_grouped = [round_weight_pair(w2_raw, u, "w2_grouped%d" % u) for u in range(2)]
        w2_pairs = [quantize_weight_pair(w2_grouped[u], "w2_%d" % u) for u in range(2)]
        for t in range(PACK):
            bank = psum.tile([P, S], F32, name="bank")
            product(bank[:], w2_pairs, t, e_codes[:], e_bytes[:])
            ye_scaled.append(keep.tile([P, S], F32, name="ye_scaled%d" % t, align_bytes=64))
            if t < YE_PLANES_ON_SCALAR:
                nc.scalar.activation(ye_scaled[t][:], bank[:], ACT.Copy, scale=unit_abs[:, t : t + 1])
            else:
                nc.vector.tensor_scalar(ye_scaled[t][:], bank[:], unit_abs[:, t : t + 1], None, ALU.mult)

        later_first_tag, later_second_tag = "w2_1_codes", "w2_1_scales"
        first_early = keep.tile([P, PACK * CHUNK], F32, name="first_early", align_bytes=64)
        first_later = keep.tile([P, PACK * CHUNK * LAST], F32, name="first_later", tag=later_first_tag, align_bytes=64)
        second_early = keep.tile([P, PACK * CHUNK], F32, name="second_early", align_bytes=64)
        second_later = keep.tile([P, PACK * CHUNK * LAST], F32, name="second_later", tag=later_second_tag, align_bytes=64)

        def chunk_planes(early, later, c):
            flat = early[:] if c == 0 else later[:, PACK * CHUNK * (c - 1) : PACK * CHUNK * c]
            return flat.rearrange("p (t r) -> p t r", t=PACK)

        firsts = [chunk_planes(first_early, first_later, c) for c in range(CHUNKS)]
        seconds = [chunk_planes(second_early, second_later, c) for c in range(CHUNKS)]
        for c in range(CHUNKS):
            for t in range(PACK):
                nc.scalar.activation(firsts[c][:, t, :], y_signed[t][:].indirect(t1_list[:, entries(c)]), ACT.Copy)
                nc.scalar.activation(seconds[c][:, t, :], y_scaled[t][:].indirect(t2_list[:, entries(c)]), ACT.Copy)
        last_fused = PACK - QW_PLANES_ON_SCALAR
        last_eq = keep.tile([P, QW_PLANES_ON_SCALAR, CHUNK], F32, name="last_eq")
        for t in range(last_fused, PACK):
            nc.scalar.activation(last_eq[:, t - last_fused, :], ye_scaled[t][:].indirect(qw_list[:, entries(LAST)]), ACT.Copy)

        w3_grouped = [round_weight_pair(w3_raw, u, "w3_grouped%d" % u) for u in range(2)]
        w3_pairs = [quantize_weight_pair(w3_grouped[u], "w3_%d" % u) for u in range(2)]

        def scaled_fq(c):
            larger = work.tile([P, PACK, CHUNK], F32, name="larger")
            fq = work.tile([P, PACK, CHUNK], F32, name="fq", bufs=1, align_bytes=64)
            for t in range(PACK):
                nc.vector.scalar_tensor_tensor(
                    larger[:, t, :], firsts[c][:, t, :], unit_tile[:, t : t + 1], seconds[c][:, t, :], ALU.mult, ALU.max
                )
            fused = last_fused if c == LAST else PACK
            for t in range(fused):
                nc.vector.tensor_tensor(
                    fq[:, t, :], ye_scaled[t][:].indirect(qw_list[:, entries(c)]), larger[:, t, :], ALU.add
                )
            if c == LAST:
                nc.vector.tensor_tensor(fq[:, fused:, :], last_eq[:], larger[:, fused:, :], ALU.add)
            return fq

        out_rows = out_0.rearrange("(p t) r -> p t r", t=PACK)
        out_words = out_1[0].rearrange("p r t -> p (r t)").bitcast(I32)

        def answer(start, width, fq, first):
            hid = work.tile([P, width * PACK], BF16, name="hid", align_bytes=64)
            nc.vector.tensor_tensor(interleaved(hid), planes_walk(fq), planes_walk(first), ALU.mult)
            codes = keep.tile([P, width], U32, name="hid_codes%d" % start, align_bytes=64)
            scales = keep.tile([P, width], U8, name="hid_scales%d" % start, align_bytes=64)
            nc.vector.quantize_mx(out=codes[:].bitcast(FP8X4), scales=scales[:], in_=hid[:])
            result = keep.tile([P, PACK, width], F32, name="result%d" % start)
            per_bank = BANK // width
            for t0 in range(0, PACK, per_bank):
                bank = psum.tile([P, per_bank, width], F32, name="bank")
                for t in range(t0, t0 + per_bank):
                    product(bank[:, t - t0, :], w3_pairs, t, codes[:], scales[:])
                held = slice(t0, t0 + per_bank)
                nc.scalar.copy(result[:, held, :], bank[:])
                nc.sync.dma_start(out_rows[:, held, start : start + width], result[:, held, :])
            return start, width, result

        pieces = []
        for c in range(CHUNKS):
            fq = scaled_fq(c)
            width = TAIL_PIECE if c == LAST else CHUNK
            for lo in range(0, CHUNK, width):
                cols = slice(lo, lo + width)
                pieces.append(answer(c * CHUNK + lo, width, fq[:, :, cols], firsts[c][:, :, cols]))

        out_scales = work.tile([P, U], U8, name="out_scales", tag="fq", bufs=1, align_bytes=64)
        out_codes = keep.tile([P, U], I32, name="out_codes", align_bytes=64)
        last_start = LAST * CHUNK
        scalar_tags = ("hid_codes%d" % (last_start - CHUNK), "hid_scales%d" % (last_start - CHUNK))
        vector_tags = (later_first_tag, later_second_tag)
        for i, (start, width, result) in enumerate(pieces):
            if i < ROUNDED_ON_SCALAR:
                copy, tag = nc.scalar.copy, scalar_tags[i]
            else:
                copy, tag = nc.vector.tensor_copy, vector_tags[i % 2]
            rounded = keep.tile([P, width * PACK], BF16, name="rounded", tag=tag, align_bytes=64)
            copy(interleaved(rounded), planes_walk(result[:]))
            cols = slice(start, start + width)
            nc.vector.quantize_mx(out=out_codes[:, cols].bitcast(FP8X4), scales=out_scales[:, cols], in_=rounded[:])
            if start + width == last_start:
                nc.sync.dma_start(out_words[:, :last_start], out_codes[:, :last_start])
            elif start + width == U:
                nc.sync.dma_start(out_words[:, last_start:], out_codes[:, last_start:])
        for r in range(PACK):
            queue = nc.sync if r % 2 == 0 else nc.scalar
            queue.dma_start(out_2[0, r::PACK, :].bitcast(I32), out_scales[r:P:QUADRANT, :].bitcast(I32))
